import numpy as np
import ml_dtypes

BF16 = ml_dtypes.bfloat16


def bf(x):
    return np.asarray(x, np.float32).astype(BF16)


def f32(x):
    return np.asarray(x, np.float32)


def f64(x):
    return np.asarray(x).astype(np.float64)


def striped(idx):
    return np.tile(idx.reshape(-1, 16).T, (8, 1))


def rows(idx, k):
    return np.tile(idx, (k, 1))


def look(tab, idx):
    return np.take_along_axis(f64(tab), rows(idx, len(tab)), axis=1)


K, S, H, V, N, M = 128, 2048, 256, 2048, 2048, 256


def setup_inputs():
    return {"z": bf(np.random.standard_normal((H, S))), "wt": bf(np.random.standard_normal((H, K)) / np.sqrt(H)), "y": f32(1.0 * np.random.standard_normal((K, V))), "w": bf(np.random.standard_normal((K, M)) / np.sqrt(K)), "b": f32(0.5 * np.random.standard_normal((M, 1))), "offs": striped(np.random.permutation(S)[:N])}


def reference(z, wt, y, w, b, offs):
    idx = offs[:16].T.reshape(-1)
    tab = f64(wt).T @ f64(z)
    x = f64(y) / (1.0 + np.exp(-look(tab, idx)))
    return np.maximum(f64(w).T @ x + f64(b), 0.0)

@@ -1,0 +1,58 @@
+import concourse.mybir as mybir
+
+BF16, F32, U16 = mybir.dt.bfloat16, mybir.dt.float32, mybir.dt.uint16
+ADD, MAX, MULT = mybir.AluOpType.add, mybir.AluOpType.max, mybir.AluOpType.mult
+SIGMOID = mybir.ActivationFunctionType.Sigmoid
+
+P = 128
+H, S, K = 256, 2048, 128
+N, M = 2048, 256
+PIECE = 512
+FLOPS = 2 * H * K * S + 2 * K * M * N
+
+
+def tile_lookup_pjsig_relu_kernel(tc, z, wt, y, w, b, offs, out):
+    nc = tc.nc
+    with (
+        tc.tile_pool(name="held", bufs=1) as held,
+        tc.tile_pool(name="work", bufs=3) as work,
+        tc.psum_pool(name="psum", bufs=4) as psum,
+    ):
+        wt_tile = held.tile([P, H // P, K], BF16, name="wt_tile")
+        z_tile = held.tile([P, H // P, S], BF16, name="z_tile")
+        offsets = held.tile([P, N // 16], U16, name="offsets")
+        y_tile = held.tile([P, N], F32, name="y_tile")
+        w_tile = held.tile([P, M], BF16, name="w_tile")
+        bias = held.tile([P, M // P], F32, name="bias")
+        tab = held.tile([P, S], F32, name="tab")
+
+        z_blocks = z.rearrange("(k p) s -> p k s", p=P)
+        nc.sync.dma_start(wt_tile[:], wt.rearrange("(k p) r -> p k r", p=P))
+        for c in range(0, S, PIECE):
+            nc.sync.dma_start(z_tile[:, :, c : c + PIECE], z_blocks[:, :, c : c + PIECE])
+        nc.sync.dma_start(offsets[:], offs)
+        for j in range(0, N, PIECE):
+            nc.sync.dma_start(y_tile[:, j : j + PIECE], y[:, j : j + PIECE])
+        nc.sync.dma_start(w_tile[:], w)
+        nc.sync.dma_start(bias[:], b.rearrange("(m p) o -> p (m o)", p=P))
+
+        for c in range(0, S, PIECE):
+            scores = psum.tile([P, PIECE], F32, name="scores")
+            for k in range(H // P):
+                nc.tensor.matmul(
+                    scores[:], wt_tile[:, k, :], z_tile[:, k, c : c + PIECE], start=(k == 0), stop=(k == H // P - 1)
+                )
+            nc.vector.tensor_copy(tab[:, c : c + PIECE], scores[:])
+
+        for j in range(0, N, PIECE):
+            picked = tab[:].indirect(offsets[:, j // 16 : (j + PIECE) // 16])
+            gate = work.tile([P, PIECE], F32, name="gate")
+            nc.scalar.activation(gate[:], picked, SIGMOID)
+            x = work.tile([P, PIECE], BF16, name="x")
+            nc.vector.tensor_tensor(x[:], gate[:], y_tile[:, j : j + PIECE], MULT)
+            for m in range(M // P):
+                layer = psum.tile([P, PIECE], F32, name="layer")
+                nc.tensor.matmul(layer[:], w_tile[:, m * P : (m + 1) * P], x[:])
+                rows = work.tile([P, PIECE], F32, name="rows")
+                nc.vector.tensor_scalar(rows[:], layer[:], bias[:, m : m + 1], 0.0, ADD, MAX)
+                nc.sync.dma_start(out[m * P : (m + 1) * P, j : j + PIECE], rows[:])

@@ -2,11 +2,12 @@ import concourse.mybir as mybir
 
 BF16, F32, U16 = mybir.dt.bfloat16, mybir.dt.float32, mybir.dt.uint16
 ADD, MAX, MULT = mybir.AluOpType.add, mybir.AluOpType.max, mybir.AluOpType.mult
-SIGMOID = mybir.ActivationFunctionType.Sigmoid
+SIGMOID, RELU = mybir.ActivationFunctionType.Sigmoid, mybir.ActivationFunctionType.Relu
 
 P = 128
 H, S, K = 256, 2048, 128
 N, M = 2048, 256
+BANK = 512
 PIECE = 512
 FLOPS = 2 * H * K * S + 2 * K * M * N
 
@@ -15,7 +16,7 @@ def tile_lookup_pjsig_relu_kernel(tc, z, wt, y, w, b, offs, out):
     nc = tc.nc
     with (
         tc.tile_pool(name="held", bufs=1) as held,
-        tc.tile_pool(name="work", bufs=3) as work,
+        tc.tile_pool(name="work", bufs=8) as work,
         tc.psum_pool(name="psum", bufs=4) as psum,
     ):
         wt_tile = held.tile([P, H // P, K], BF16, name="wt_tile")
@@ -26,33 +27,60 @@ def tile_lookup_pjsig_relu_kernel(tc, z, wt, y, w, b, offs, out):
         bias = held.tile([P, M // P], F32, name="bias")
         tab = held.tile([P, S], F32, name="tab")
 
+        zeros = held.tile([P, BANK], BF16, name="zeros")
+        nc.gpsimd.memset(zeros[:], 0.0)
+        warm = held.tile([P, 1], F32, name="warm")
+        nc.scalar.activation(warm[:], zeros[:, 0:1], SIGMOID)
+        for i in range(3):
+            idle = psum.tile([P, BANK], F32, name="idle", tag="scores")
+            nc.tensor.matmul(idle[:], zeros[:, 0:P], zeros[:])
+
         z_blocks = z.rearrange("(k p) s -> p k s", p=P)
-        nc.sync.dma_start(wt_tile[:], wt.rearrange("(k p) r -> p k r", p=P))
-        for c in range(0, S, PIECE):
-            nc.sync.dma_start(z_tile[:, :, c : c + PIECE], z_blocks[:, :, c : c + PIECE])
+        nc.scalar.dma_start(wt_tile[:], wt.rearrange("(k p) r -> p k r", p=P))
+        for c in range(0, S, 512):
+            nc.sync.dma_start(z_tile[:, :, c : c + 512], z_blocks[:, :, c : c + 512])
         nc.sync.dma_start(offsets[:], offs)
-        for j in range(0, N, PIECE):
-            nc.sync.dma_start(y_tile[:, j : j + PIECE], y[:, j : j + PIECE])
+        for j in range(0, N, BANK):
+            nc.sync.dma_start(y_tile[:, j : j + BANK], y[:, j : j + BANK])
         nc.sync.dma_start(w_tile[:], w)
         nc.sync.dma_start(bias[:], b.rearrange("(m p) o -> p (m o)", p=P))
 
-        for c in range(0, S, PIECE):
-            scores = psum.tile([P, PIECE], F32, name="scores")
+        for c in range(0, S, BANK):
+            scores = psum.tile([P, BANK], F32, name="scores")
             for k in range(H // P):
                 nc.tensor.matmul(
-                    scores[:], wt_tile[:, k, :], z_tile[:, k, c : c + PIECE], start=(k == 0), stop=(k == H // P - 1)
+                    scores[:], wt_tile[:, k, :], z_tile[:, k, c : c + BANK], start=(k == 0), stop=(k == H // P - 1)
                 )
-            nc.vector.tensor_copy(tab[:, c : c + PIECE], scores[:])
+            half = c + BANK // 2
+            nc.vector.tensor_copy(tab[:, c:half], scores[:, : BANK // 2])
+            nc.scalar.copy(tab[:, half : c + BANK], scores[:, BANK // 2 :])
 
-        for j in range(0, N, PIECE):
+        def look_up(j):
             picked = tab[:].indirect(offsets[:, j // 16 : (j + PIECE) // 16])
             gate = work.tile([P, PIECE], F32, name="gate")
             nc.scalar.activation(gate[:], picked, SIGMOID)
             x = work.tile([P, PIECE], BF16, name="x")
-            nc.vector.tensor_tensor(x[:], gate[:], y_tile[:, j : j + PIECE], MULT)
+            engine = nc.vector if j in (0, N - PIECE) else nc.gpsimd
+            engine.tensor_tensor(x[:], gate[:], y_tile[:, j : j + PIECE], MULT)
+            return x
+
+        def layer(j, x):
             for m in range(M // P):
-                layer = psum.tile([P, PIECE], F32, name="layer")
-                nc.tensor.matmul(layer[:], w_tile[:, m * P : (m + 1) * P], x[:])
+                product = psum.tile([P, PIECE], F32, name="product")
+                nc.tensor.matmul(product[:], w_tile[:, m * P : (m + 1) * P], x[:])
                 rows = work.tile([P, PIECE], F32, name="rows")
-                nc.vector.tensor_scalar(rows[:], layer[:], bias[:, m : m + 1], 0.0, ADD, MAX)
-                nc.sync.dma_start(out[m * P : (m + 1) * P, j : j + PIECE], rows[:])
+                if m == 1 and j + 3 * PIECE >= N:
+                    store = nc.scalar
+                    nc.scalar.activation(rows[:], product[:], RELU, bias=bias[:, m : m + 1])
+                else:
+                    store = nc.sync
+                    nc.vector.tensor_scalar(rows[:], product[:], bias[:, m : m + 1], 0.0, ADD, MAX)
+                store.dma_start(out[m * P : (m + 1) * P, j : j + PIECE], rows[:])
+
+        pieces = list(range(0, N, PIECE))
+        x = {}
+        for i in range(len(pieces) + 2):
+            if i < len(pieces):
+                x[i] = look_up(pieces[i])
+            if i >= 2:
+                layer(pieces[i - 2], x[i - 2])

@@ -8,7 +8,7 @@ P = 128
 H, S, K = 256, 2048, 128
 N, M = 2048, 256
 BANK = 512
-PIECE = 512
+PIECE = 256
 FLOPS = 2 * H * K * S + 2 * K * M * N
 
 
@@ -16,13 +16,12 @@ def tile_lookup_pjsig_relu_kernel(tc, z, wt, y, w, b, offs, out):
     nc = tc.nc
     with (
         tc.tile_pool(name="held", bufs=1) as held,
+        tc.tile_pool(name="stream", bufs=4) as stream,
         tc.tile_pool(name="work", bufs=8) as work,
         tc.psum_pool(name="psum", bufs=4) as psum,
     ):
         wt_tile = held.tile([P, H // P, K], BF16, name="wt_tile")
-        z_tile = held.tile([P, H // P, S], BF16, name="z_tile")
         offsets = held.tile([P, N // 16], U16, name="offsets")
-        y_tile = held.tile([P, N], F32, name="y_tile")
         w_tile = held.tile([P, M], BF16, name="w_tile")
         bias = held.tile([P, M // P], F32, name="bias")
         tab = held.tile([P, S], F32, name="tab")
@@ -37,11 +36,12 @@ def tile_lookup_pjsig_relu_kernel(tc, z, wt, y, w, b, offs, out):
 
         z_blocks = z.rearrange("(k p) s -> p k s", p=P)
         nc.scalar.dma_start(wt_tile[:], wt.rearrange("(k p) r -> p k r", p=P))
-        for c in range(0, S, 512):
-            nc.sync.dma_start(z_tile[:, :, c : c + 512], z_blocks[:, :, c : c + 512])
+        z_tiles = []
+        for c in range(0, S, BANK):
+            z_tile = stream.tile([P, H // P, BANK], BF16, name="z_tile", tag="stream")
+            nc.sync.dma_start(z_tile[:], z_blocks[:, :, c : c + BANK])
+            z_tiles.append(z_tile)
         nc.sync.dma_start(offsets[:], offs)
-        for j in range(0, N, BANK):
-            nc.sync.dma_start(y_tile[:, j : j + BANK], y[:, j : j + BANK])
         nc.sync.dma_start(w_tile[:], w)
         nc.sync.dma_start(bias[:], b.rearrange("(m p) o -> p (m o)", p=P))
 
@@ -49,33 +49,39 @@ def tile_lookup_pjsig_relu_kernel(tc, z, wt, y, w, b, offs, out):
             scores = psum.tile([P, BANK], F32, name="scores")
             for k in range(H // P):
                 nc.tensor.matmul(
-                    scores[:], wt_tile[:, k, :], z_tile[:, k, c : c + BANK], start=(k == 0), stop=(k == H // P - 1)
+                    scores[:], wt_tile[:, k, :], z_tiles[c // BANK][:, k, :], start=(k == 0), stop=(k == H // P - 1)
                 )
             half = c + BANK // 2
             nc.vector.tensor_copy(tab[:, c:half], scores[:, : BANK // 2])
             nc.scalar.copy(tab[:, half : c + BANK], scores[:, BANK // 2 :])
+
+        y_tiles = []
+        for j in range(0, N, BANK):
+            y_tile = stream.tile([P, BANK], F32, name="y_tile", tag="stream")
+            nc.sync.dma_start(y_tile[:], y[:, j : j + BANK])
+            y_tiles.append(y_tile)
 
         def look_up(j):
             picked = tab[:].indirect(offsets[:, j // 16 : (j + PIECE) // 16])
             gate = work.tile([P, PIECE], F32, name="gate")
             nc.scalar.activation(gate[:], picked, SIGMOID)
             x = work.tile([P, PIECE], BF16, name="x")
-            engine = nc.vector if j in (0, N - PIECE) else nc.gpsimd
-            engine.tensor_tensor(x[:], gate[:], y_tile[:, j : j + PIECE], MULT)
+            engine = nc.vector
+            engine.tensor_tensor(x[:], gate[:], y_tiles[j // BANK][:, j % BANK : j % BANK + PIECE], MULT)
             return x
 
+        out_blocks = out.rearrange("(m p) j -> p m j", p=P)
+
         def layer(j, x):
+            rows = work.tile([P, M // P, PIECE], F32, name="rows")
             for m in range(M // P):
                 product = psum.tile([P, PIECE], F32, name="product")
                 nc.tensor.matmul(product[:], w_tile[:, m * P : (m + 1) * P], x[:])
-                rows = work.tile([P, PIECE], F32, name="rows")
-                if m == 1 and j + 3 * PIECE >= N:
-                    store = nc.scalar
-                    nc.scalar.activation(rows[:], product[:], RELU, bias=bias[:, m : m + 1])
+                if m == 1 and j + 2 * PIECE >= N:
+                    nc.scalar.activation(rows[:, m, :], product[:], RELU, bias=bias[:, m : m + 1])
                 else:
-                    store = nc.sync
-                    nc.vector.tensor_scalar(rows[:], product[:], bias[:, m : m + 1], 0.0, ADD, MAX)
-                store.dma_start(out[m * P : (m + 1) * P, j : j + PIECE], rows[:])
+                    nc.vector.tensor_scalar(rows[:, m, :], product[:], bias[:, m : m + 1], 0.0, ADD, MAX)
+            nc.sync.dma_start(out_blocks[:, :, j : j + PIECE], rows[:])
 
         pieces = list(range(0, N, PIECE))
         x = {}

@@ -7,7 +7,7 @@ SIGMOID, RELU = mybir.ActivationFunctionType.Sigmoid, mybir.ActivationFunctionTy
 P = 128
 H, S, K = 256, 2048, 128
 N, M = 2048, 256
-BANK = 512
+LOAD = 512
 PIECE = 256
 FLOPS = 2 * H * K * S + 2 * K * M * N
 
@@ -16,9 +16,9 @@ def tile_lookup_pjsig_relu_kernel(tc, z, wt, y, w, b, offs, out):
     nc = tc.nc
     with (
         tc.tile_pool(name="held", bufs=1) as held,
-        tc.tile_pool(name="stream", bufs=4) as stream,
-        tc.tile_pool(name="work", bufs=8) as work,
-        tc.psum_pool(name="psum", bufs=4) as psum,
+        tc.tile_pool(name="stream", bufs=S // LOAD) as stream,
+        tc.tile_pool(name="work", bufs=N // PIECE) as work,
+        tc.psum_pool(name="psum", bufs=8) as psum,
     ):
         wt_tile = held.tile([P, H // P, K], BF16, name="wt_tile")
         offsets = held.tile([P, N // 16], U16, name="offsets")
@@ -26,39 +26,41 @@ def tile_lookup_pjsig_relu_kernel(tc, z, wt, y, w, b, offs, out):
         bias = held.tile([P, M // P], F32, name="bias")
         tab = held.tile([P, S], F32, name="tab")
 
-        zeros = held.tile([P, BANK], BF16, name="zeros")
+        zeros = held.tile([P, PIECE], BF16, name="zeros")
         nc.gpsimd.memset(zeros[:], 0.0)
         warm = held.tile([P, 1], F32, name="warm")
         nc.scalar.activation(warm[:], zeros[:, 0:1], SIGMOID)
-        for i in range(3):
-            idle = psum.tile([P, BANK], F32, name="idle", tag="scores")
+        idle = psum.tile([P, PIECE], F32, name="idle", tag="bank")
+        for i in range(8):
             nc.tensor.matmul(idle[:], zeros[:, 0:P], zeros[:])
 
-        z_blocks = z.rearrange("(k p) s -> p k s", p=P)
-        nc.scalar.dma_start(wt_tile[:], wt.rearrange("(k p) r -> p k r", p=P))
+        z_pairs = z.rearrange("(p k) s -> p k s", p=P)
+        nc.scalar.dma_start(wt_tile[:], wt.rearrange("(p k) r -> p k r", p=P))
         z_tiles = []
-        for c in range(0, S, BANK):
-            z_tile = stream.tile([P, H // P, BANK], BF16, name="z_tile", tag="stream")
-            nc.sync.dma_start(z_tile[:], z_blocks[:, :, c : c + BANK])
+        for c in range(0, S, LOAD):
+            z_tile = stream.tile([P, H // P, LOAD], BF16, name="z_tile", tag="stream")
+            nc.sync.dma_start(z_tile[:], z_pairs[:, :, c : c + LOAD])
             z_tiles.append(z_tile)
         nc.sync.dma_start(offsets[:], offs)
         nc.sync.dma_start(w_tile[:], w)
         nc.sync.dma_start(bias[:], b.rearrange("(m p) o -> p (m o)", p=P))
 
-        for c in range(0, S, BANK):
-            scores = psum.tile([P, BANK], F32, name="scores")
+        for c in range(0, S, PIECE):
+            z_tile, first = z_tiles[c // LOAD], c % LOAD
+            scores = psum.tile([P, PIECE], F32, name="scores", tag="bank")
             for k in range(H // P):
                 nc.tensor.matmul(
-                    scores[:], wt_tile[:, k, :], z_tiles[c // BANK][:, k, :], start=(k == 0), stop=(k == H // P - 1)
+                    scores[:], wt_tile[:, k, :], z_tile[:, k, first : first + PIECE], start=(k == 0), stop=(k == 1)
                 )
-            half = c + BANK // 2
-            nc.vector.tensor_copy(tab[:, c:half], scores[:, : BANK // 2])
-            nc.scalar.copy(tab[:, half : c + BANK], scores[:, BANK // 2 :])
+            if (c // PIECE) % 2 == 0:
+                nc.vector.tensor_copy(tab[:, c : c + PIECE], scores[:])
+            else:
+                nc.scalar.copy(tab[:, c : c + PIECE], scores[:])
 
         y_tiles = []
-        for j in range(0, N, BANK):
-            y_tile = stream.tile([P, BANK], F32, name="y_tile", tag="stream")
-            nc.sync.dma_start(y_tile[:], y[:, j : j + BANK])
+        for j in range(0, N, LOAD):
+            y_tile = stream.tile([P, LOAD], F32, name="y_tile", tag="stream")
+            nc.sync.dma_start(y_tile[:], y[:, j : j + LOAD])
             y_tiles.append(y_tile)
 
         def look_up(j):
@@ -67,7 +69,7 @@ def tile_lookup_pjsig_relu_kernel(tc, z, wt, y, w, b, offs, out):
             nc.scalar.activation(gate[:], picked, SIGMOID)
             x = work.tile([P, PIECE], BF16, name="x")
             engine = nc.vector
-            engine.tensor_tensor(x[:], gate[:], y_tiles[j // BANK][:, j % BANK : j % BANK + PIECE], MULT)
+            engine.tensor_tensor(x[:], gate[:], y_tiles[j // LOAD][:, j % LOAD : j % LOAD + PIECE], MULT)
             return x
 
         out_blocks = out.rearrange("(m p) j -> p m j", p=P)
@@ -75,9 +77,9 @@ def tile_lookup_pjsig_relu_kernel(tc, z, wt, y, w, b, offs, out):
         def layer(j, x):
             rows = work.tile([P, M // P, PIECE], F32, name="rows")
             for m in range(M // P):
-                product = psum.tile([P, PIECE], F32, name="product")
+                product = psum.tile([P, PIECE], F32, name="product", tag="bank")
                 nc.tensor.matmul(product[:], w_tile[:, m * P : (m + 1) * P], x[:])
-                if m == 1 and j + 2 * PIECE >= N:
+                if m == 1 and j + 3 * PIECE >= N:
                     nc.scalar.activation(rows[:, m, :], product[:], RELU, bias=bias[:, m : m + 1])
                 else:
                     nc.vector.tensor_scalar(rows[:, m, :], product[:], bias[:, m : m + 1], 0.0, ADD, MAX)

import concourse.mybir as mybir

BF16, F32, U16 = mybir.dt.bfloat16, mybir.dt.float32, mybir.dt.uint16
ADD, MAX, MULT = mybir.AluOpType.add, mybir.AluOpType.max, mybir.AluOpType.mult
SIGMOID, RELU = mybir.ActivationFunctionType.Sigmoid, mybir.ActivationFunctionType.Relu

P = 128
H, S, K = 256, 2048, 128
N, M = 2048, 256
LOAD = 512
PIECE = 256
FLOPS = 2 * H * K * S + 2 * K * M * N


def tile_lookup_pjsig_relu_kernel(tc, z, wt, y, w, b, offs, out):
    nc = tc.nc
    with (
        tc.tile_pool(name="held", bufs=1) as held,
        tc.tile_pool(name="stream", bufs=S // LOAD) as stream,
        tc.tile_pool(name="work", bufs=N // PIECE) as work,
        tc.psum_pool(name="psum", bufs=8) as psum,
    ):
        wt_tile = held.tile([P, H // P, K], BF16, name="wt_tile")
        offsets = held.tile([P, N // 16], U16, name="offsets")
        w_tile = held.tile([P, M], BF16, name="w_tile")
        bias = held.tile([P, M // P], F32, name="bias")
        tab = held.tile([P, S], F32, name="tab")

        zeros = held.tile([P, PIECE], BF16, name="zeros")
        nc.gpsimd.memset(zeros[:], 0.0)
        warm = held.tile([P, 1], F32, name="warm")
        nc.scalar.activation(warm[:], zeros[:, 0:1], SIGMOID)
        idle = psum.tile([P, PIECE], F32, name="idle", tag="bank")
        for i in range(8):
            nc.tensor.matmul(idle[:], zeros[:, 0:P], zeros[:])

        z_pairs = z.rearrange("(p k) s -> p k s", p=P)
        nc.scalar.dma_start(wt_tile[:], wt.rearrange("(p k) r -> p k r", p=P))
        z_tiles = []
        for c in range(0, S, LOAD):
            z_tile = stream.tile([P, H // P, LOAD], BF16, name="z_tile", tag="stream")
            nc.sync.dma_start(z_tile[:], z_pairs[:, :, c : c + LOAD])
            z_tiles.append(z_tile)
        nc.sync.dma_start(offsets[:], offs)
        nc.sync.dma_start(w_tile[:], w)
        nc.sync.dma_start(bias[:], b.rearrange("(m p) o -> p (m o)", p=P))

        for c in range(0, S, PIECE):
            z_tile, first = z_tiles[c // LOAD], c % LOAD
            scores = psum.tile([P, PIECE], F32, name="scores", tag="bank")
            for k in range(H // P):
                nc.tensor.matmul(
                    scores[:], wt_tile[:, k, :], z_tile[:, k, first : first + PIECE], start=(k == 0), stop=(k == 1)
                )
            if (c // PIECE) % 2 == 0:
                nc.vector.tensor_copy(tab[:, c : c + PIECE], scores[:])
            else:
                nc.scalar.copy(tab[:, c : c + PIECE], scores[:])

        y_tiles = []
        for j in range(0, N, LOAD):
            y_tile = stream.tile([P, LOAD], F32, name="y_tile", tag="stream")
            nc.sync.dma_start(y_tile[:], y[:, j : j + LOAD])
            y_tiles.append(y_tile)

        def look_up(j):
            picked = tab[:].indirect(offsets[:, j // 16 : (j + PIECE) // 16])
            gate = work.tile([P, PIECE], F32, name="gate")
            nc.scalar.activation(gate[:], picked, SIGMOID)
            x = work.tile([P, PIECE], BF16, name="x")
            engine = nc.vector
            engine.tensor_tensor(x[:], gate[:], y_tiles[j // LOAD][:, j % LOAD : j % LOAD + PIECE], MULT)
            return x

        out_blocks = out.rearrange("(m p) j -> p m j", p=P)

        def layer(j, x):
            rows = work.tile([P, M // P, PIECE], F32, name="rows")
            for m in range(M // P):
                product = psum.tile([P, PIECE], F32, name="product", tag="bank")
                nc.tensor.matmul(product[:], w_tile[:, m * P : (m + 1) * P], x[:])
                if m == 1 and j + 3 * PIECE >= N:
                    nc.scalar.activation(rows[:, m, :], product[:], RELU, bias=bias[:, m : m + 1])
                else:
                    nc.vector.tensor_scalar(rows[:, m, :], product[:], bias[:, m : m + 1], 0.0, ADD, MAX)
            nc.sync.dma_start(out_blocks[:, :, j : j + PIECE], rows[:])

        pieces = list(range(0, N, PIECE))
        x = {}
        for i in range(len(pieces) + 2):
            if i < len(pieces):
                x[i] = look_up(pieces[i])
            if i >= 2:
                layer(pieces[i - 2], x[i - 2])
